import numpy as np
import ml_dtypes


def mxq(x, axis, fmt="e4m3"):
    dtype, down = {"e4m3": (ml_dtypes.float8_e4m3fn, 7), "e5m2": (ml_dtypes.float8_e5m2, 14)}[fmt]
    v = np.moveaxis(np.asarray(x, np.float32).astype(ml_dtypes.bfloat16).astype(np.float64), axis, -1)
    blocks = v.reshape(v.shape[:-1] + (-1, 32))
    amax = np.abs(blocks).max(-1, keepdims=True)
    byte = np.maximum(np.where(amax > 0, np.frexp(amax)[1] - 1 + 127, 0) - down, 1)
    scale = np.exp2(byte - 127.0)
    codes = (blocks / scale).astype(np.float32).astype(dtype).astype(np.float64)
    return np.moveaxis((codes * scale).reshape(v.shape), -1, axis)


WIDE = False


def mx_kscale(k):
    if not WIDE:
        return np.ones(k)
    levels = np.array([10, -10, 5, -5, 0])
    if k % 512:
        return np.exp2(np.random.permutation(np.resize(levels, k // 32))).repeat(32)
    a = np.empty((k // 512, 16))
    for p in range(k // 512):
        a[p, :8] = np.random.permutation(np.resize(levels, 8))
        for g in range(8):
            far = levels[np.abs(levels - a[p, g]) >= 10]
            a[p, g + 8] = far[np.random.randint(len(far))]
    return np.exp2(a.ravel()).repeat(32)


def f64(x):
    return np.asarray(x).astype(np.float64)


def striped(idx):
    return np.tile(idx.reshape(-1, 16).T, (8, 1)).astype(np.uint16)


def unstriped(offs):
    return offs[:16].T.reshape(-1).astype(np.int64)


def striped8(idx):
    return np.concatenate([x.reshape(-1, 16).T for x in idx]).astype(np.uint16)


def runs(offs, k):
    lists = np.stack([offs[16 * r : 16 * r + 16].T.reshape(-1) for r in range(8)]).astype(np.int64)
    return lists[np.arange(k) % 512 // 64]


def pack_weight(w):
    k, n = w.shape
    w = f64(np.asarray(w, np.float32).astype(ml_dtypes.bfloat16)).reshape(k // 32, 32, n)
    amax = np.abs(w).max(1)
    byte = np.clip(np.where(amax > 0, np.frexp(amax)[1] - 1 + 127 - 7, 1), 1, 254)
    scaled = (w * np.exp2(127.0 - byte)[:, None, :]).reshape(k, n).astype(np.float32)
    words = np.ascontiguousarray(scaled.reshape(k // 512, 128, 4, n).transpose(0, 1, 3, 2)).astype(ml_dtypes.float8_e4m3fn).view(np.uint8)
    return words, np.ascontiguousarray(byte.astype(np.uint8).reshape(k // 512, 16, n))


def unpack_weight(words, scales):
    g, p, n, _ = words.shape
    vals = np.ascontiguousarray(words).view(ml_dtypes.float8_e4m3fn).astype(np.float64) * np.repeat(np.exp2(scales.astype(np.float64) - 127.0), 8, axis=1)[..., None]
    return vals.transpose(0, 1, 3, 2).reshape(g * 512, n)


def sigmoid(v):
    return 1.0 / (1.0 + np.exp(-np.maximum(v, -700.0)))


K, T, S, N, H, W = 512, 2048, 512, 512, 512, 256


def setup_inputs():
    n = np.random.standard_normal
    s = mx_kscale(K)[:, None]
    u = mx_kscale(S)
    packed_xT = pack_weight(n((K, T)) * s)
    perm = np.stack([np.random.permutation(H) for _ in range(8)])
    return {
        "x_words": packed_xT[0],
        "x_scales": packed_xT[1],
        "wa": (n((K, H)) / np.sqrt(K) / s).astype(np.float32),
        "wb": (n((K, N)) / np.sqrt(K) / s).astype(np.float32),
        "gt": (np.random.uniform(0.5, 1.5, (S, 1)) * u[:, None]).astype(np.float32),
        "gi": (np.random.uniform(0.5, 1.5, (S, 1)) / u[:, None]).astype(np.float32),
        "offs": striped(np.random.permutation(T)[:S]),
        "two": striped(np.random.permutation(T)[:S]),
        "n1": striped8(perm[:, :W]),
        "n2": striped8(perm[:, W:]),
        "n3": striped8(np.stack([np.random.permutation(N) for _ in range(8)])),
        "n4": striped8(np.stack([np.random.permutation(N) for _ in range(8)])),
    }


def reference(x_words, x_scales, wa, wb, gt, gi, offs, two, n1, n2, n3, n4):
    xq = unpack_weight(x_words, x_scales)[:, unstriped(offs)]
    a = xq.T @ mxq(f64(wa), 0, "e4m3")
    pa = a[np.arange(S)[:, None], runs(n1, S)]
    pb = a[np.arange(S)[:, None], runs(n2, S)]
    rb = pa - pb
    ra = 0.75 * (pa + pb)
    ds = np.zeros((S, H))
    ds[np.arange(S)[:, None], runs(n1, S)] = ra
    dt = ds.copy()
    dt[np.arange(S)[:, None], runs(n2, S)] = rb
    z = f64(gt) * dt
    x_two = unpack_weight(x_words, x_scales)[:, unstriped(two)]
    b = x_two.T @ mxq(f64(wb), 0, "e4m3")
    z2 = f64(gi) * b
    cv = 0.0625 * ((mxq(z, 0, "e4m3").T @ mxq(z2, 0, "e4m3")))
    return (cv - (cv[np.arange(H)[:, None], runs(n3, H)])) * (sigmoid(cv[np.arange(H)[:, None], runs(n4, H)]))

@@ -1,0 +1,251 @@
+from contextlib import ExitStack
+
+import concourse.mybir as mybir
+
+K, T, S, N, H, W = 512, 2048, 512, 512, 512, 256
+FLOPS = 2 * K * S * H + 2 * K * S * N + 2 * S * H * N
+
+F32 = mybir.dt.float32
+BF16 = mybir.dt.bfloat16
+I32 = mybir.dt.int32
+U32 = mybir.dt.uint32
+U16 = mybir.dt.uint16
+U8 = mybir.dt.uint8
+FP8X4 = mybir.dt.float8_e4m3fn_x4
+ALU = mybir.AluOpType
+ACT = mybir.ActivationFunctionType
+
+P = 128
+PACK = 4
+WA_CHUNKS = ((0, 256), (256, 512))
+WB_CHUNKS = ((0, 256), (256, 512))
+
+
+def weave_views(grouped, planes):
+    return (
+        grouped.rearrange("p (c i) j -> p c j i", i=PACK),
+        planes.rearrange("p j (c i) -> p c j i", i=PACK),
+    )
+
+
+def quantize(nc, codes, scales, grouped):
+    nc.vector.quantize_mx(out=codes.bitcast(FP8X4), scales=scales, in_=grouped.rearrange("p c j -> p (c j)"))
+
+
+def product(nc, acc, lhs_codes, lhs_scales, rhs_codes, rhs_scales):
+    nc.tensor.matmul_mx(
+        out=acc,
+        lhsT=lhs_codes.bitcast(FP8X4),
+        lhsT_scale=lhs_scales,
+        rhs=rhs_codes.bitcast(FP8X4),
+        rhs_scale=rhs_scales,
+        start=True,
+        stop=True,
+    )
+
+
+def tile_picked_momhaargdif_none_p_kernel(
+    tc, x_words, x_scales, wa, wb, gt, gi, offs, two, n1, n2, n3, n4, out
+):
+    nc = tc.nc
+    with ExitStack() as ctx:
+        keep = ctx.enter_context(tc.tile_pool(name="keep", bufs=1))
+        ring = ctx.enter_context(tc.tile_pool(name="ring", bufs=4))
+        psum = ctx.enter_context(tc.psum_pool(name="psum", bufs=4))
+
+        def load_list(name, src):
+            tile = keep.tile(list(src.shape), U16, name=name)
+            nc.sync.dma_start(tile[:], src)
+            return tile
+
+        def load_weights(name, w, c0, c1):
+            raw = keep.tile([P, PACK, c1 - c0], F32, name=name)
+            nc.sync.dma_start(raw[:], w.rearrange("(p j) c -> p j c", j=PACK)[:, :, c0:c1])
+            return raw
+
+        def load_column(name, g):
+            tile = keep.tile([P, PACK], F32, name=name)
+            nc.sync.dma_start(tile[:], g.rearrange("(p t) o -> p (t o)", t=PACK))
+            return tile
+
+        table_scales = keep.tile([P, T], U8, name="table_scales")
+        nc.vector.memset(table_scales[:].bitcast(I32), 0)
+        offs_t = load_list("offs_t", offs)
+        wa_raw = [load_weights("wa_raw0", wa, *WA_CHUNKS[0])]
+        for q in range(4):
+            nc.sync.dma_start(
+                table_scales[32 * q : 32 * q + 4, :].bitcast(I32), x_scales[0, 4 * q : 4 * q + 4, :].bitcast(I32)
+            )
+        wa_raw.append(load_weights("wa_raw1", wa, *WA_CHUNKS[1]))
+        two_t = load_list("two_t", two)
+        table_words = keep.tile([P, T], U32, name="table_words")
+        nc.sync.dma_start(table_words[:].bitcast(I32), x_words[0].rearrange("p n t -> p (n t)").bitcast(I32))
+        wb_raw = [load_weights("wb_raw0", wb, *WB_CHUNKS[0])]
+        gt_t = load_column("gt_t", gt)
+        n1_t = load_list("n1_t", n1)
+        n2_t = load_list("n2_t", n2)
+        wb_raw.append(load_weights("wb_raw1", wb, *WB_CHUNKS[1]))
+        gi_t = load_column("gi_t", gi)
+        n3_t = load_list("n3_t", n3)
+        n4_t = load_list("n4_t", n4)
+        three_quarters = keep.tile([P, W], F32, name="three_quarters")
+        nc.gpsimd.memset(three_quarters[:], 0.75)
+
+        def pick(name, dtype, table, lst):
+            tile = keep.tile([P, S], dtype, name=name, align_bytes=64)
+            nc.vector.tensor_copy(tile[:].rearrange("p (t m) -> p m t", t=PACK), table[:].indirect(lst[:]))
+            return tile
+
+        wa_codes = keep.tile([P, H], U32, name="wa_codes", align_bytes=64)
+        wa_scales = keep.tile([P, H], U8, name="wa_scales", align_bytes=64)
+        wa_grouped = [
+            keep.tile([P, c1 - c0, PACK], BF16, name="wa_grouped%d" % c, align_bytes=64)
+            for c, (c0, c1) in enumerate(WA_CHUNKS)
+        ]
+        for c in range(len(WA_CHUNKS)):
+            nc.scalar.copy(*weave_views(wa_grouped[c][:], wa_raw[c][:]))
+        xa_scales = pick("xa_scales", U8, table_scales, offs_t)
+        xb_scales = pick("xb_scales", U8, table_scales, two_t)
+        for c, (c0, c1) in enumerate(WA_CHUNKS):
+            quantize(nc, wa_codes[:, c0:c1], wa_scales[:, c0:c1], wa_grouped[c][:])
+        xa_words = pick("xa_words", U32, table_words, offs_t)
+        xb_words = pick("xb_words", U32, table_words, two_t)
+
+        a_acc = [psum.tile([P, H], F32, name="a_acc0", tag="first_chain", bufs=1)]
+        a_acc.extend(psum.tile([P, H], F32, name="a_acc%d" % t, tag="first", bufs=3) for t in range(1, PACK))
+        for t in range(PACK):
+            cols = slice(t * P, (t + 1) * P)
+            product(nc, a_acc[t][:], xa_words[:, cols], xa_scales[:, cols], wa_codes[:], wa_scales[:])
+
+        z_rows = [keep.tile([P, H], F32, name="z_rows%d" % t) for t in range(PACK)]
+
+        pa = [keep.tile([P, 2, W], F32, name="pa%d" % g) for g in range(2)]
+        minus_pb = [keep.tile([P, 2, W], F32, name="minus_pb%d" % g) for g in range(2)]
+        pair_sum = [keep.tile([P, 2, W], F32, name="pair_sum%d" % g) for g in range(2)]
+
+        def fetch_pairs(t):
+            g, i = divmod(t, 2)
+            if g == 0:
+                a_rows = keep.tile([P, H], F32, name="a_rows%d" % t)
+            else:
+                a_rows = keep.tile([P, H], F32, name="a_rows%d" % t, tag="wb_raw%d" % i)
+            nc.scalar.activation(a_rows[:], a_acc[t][:], ACT.Copy, scale=gt_t[:, t : t + 1])
+            nc.scalar.activation(pa[g][:, i, :], a_rows[:].indirect(n1_t[:]), ACT.Copy)
+            if t == 0:
+                nc.vector.tensor_scalar(minus_pb[g][:, i, :], a_rows[:].indirect(n2_t[:]), -1.0, 0.0, ALU.mult, ALU.add)
+            else:
+                nc.scalar.activation(minus_pb[g][:, i, :], a_rows[:].indirect(n2_t[:]), ACT.Copy, scale=-1.0)
+
+        def put_difference(t):
+            g, i = divmod(t, 2)
+            nc.vector.tensor_tensor(z_rows[t][:].indirect(n2_t[:]), pa[g][:, i, :], minus_pb[g][:, i, :], ALU.add)
+
+        scaled_pb = keep.tile([P, 2, W], F32, name="scaled_pb")
+
+        def put_sum(t):
+            g, i = divmod(t, 2)
+            other = scaled_pb[:, i, :] if g == 1 else three_quarters[:]
+            op = ALU.add if g == 1 else ALU.mult
+            nc.vector.tensor_tensor(z_rows[t][:].indirect(n1_t[:]), pair_sum[g][:, i, :], other, op)
+
+        def put_pairs(g):
+            put_difference(2 * g)
+            if g == 1:
+                nc.scalar.activation(pair_sum[g][:], pa[g][:], ACT.Copy, scale=0.75)
+                nc.scalar.activation(scaled_pb[:], minus_pb[g][:], ACT.Copy, scale=-0.75)
+            else:
+                nc.vector.tensor_tensor(pair_sum[g][:], pa[g][:], minus_pb[g][:], ALU.subtract)
+            put_difference(2 * g + 1)
+            put_sum(2 * g)
+            put_sum(2 * g + 1)
+
+        def round_z(t, u):
+            nc.scalar.copy(z_planes[:, t, u * P : (u + 1) * P], z_rows[t][:, u::PACK])
+
+        def round_z_all(t):
+            nc.scalar.copy(
+                z_planes[:, t, :].rearrange("p (u m) -> p u m", u=PACK), z_rows[t][:].rearrange("p (m u) -> p u m", u=PACK)
+            )
+
+        wb_codes = keep.tile([P, N], U32, name="wb_codes", align_bytes=64)
+        wb_scales = keep.tile([P, N], U8, name="wb_scales", align_bytes=64)
+        wb_grouped = [
+            keep.tile([P, c1 - c0, PACK], BF16, name="wb_grouped%d" % c, align_bytes=64)
+            for c, (c0, c1) in enumerate(WB_CHUNKS)
+        ]
+        b_acc = [psum.tile([P, N], F32, name="b_acc%d" % t, tag="second") for t in range(PACK)]
+
+        def prepare_wb(c):
+            c0, c1 = WB_CHUNKS[c]
+            nc.scalar.copy(*weave_views(wb_grouped[c][:], wb_raw[c][:]))
+            quantize(nc, wb_codes[:, c0:c1], wb_scales[:, c0:c1], wb_grouped[c][:])
+
+        def make_z2(c):
+            c0, c1 = WB_CHUNKS[c]
+            for t in range(PACK):
+                cols = slice(t * P, (t + 1) * P)
+                product(nc, b_acc[t][:, c0:c1], xb_words[:, cols], xb_scales[:, cols], wb_codes[:, c0:c1], wb_scales[:, c0:c1])
+                nc.scalar.activation(z2_planes[:, t, c0:c1], b_acc[t][:, c0:c1], ACT.Copy, scale=gi_t[:, t : t + 1])
+            nc.scalar.copy(*weave_views(z2_grouped[:, c0:c1, :], z2_planes[:, :, c0:c1]))
+
+        z2_planes = keep.tile([P, PACK, N], BF16, name="z2_planes")
+        z2_grouped = keep.tile([P, N, PACK], BF16, name="z2_grouped", align_bytes=64)
+        z2_codes = keep.tile([P, N], U32, name="z2_codes", align_bytes=64)
+        z2_scales = keep.tile([P, N], U8, name="z2_scales", align_bytes=64)
+
+        prepare_wb(0)
+        fetch_pairs(0)
+        fetch_pairs(1)
+        prepare_wb(1)
+        put_pairs(0)
+        fetch_pairs(2)
+        fetch_pairs(3)
+        put_pairs(1)
+        make_z2(0)
+        make_z2(1)
+        z_planes = keep.tile([P, PACK, H], BF16, name="z_planes", tag="z2_planes")
+        for t in range(PACK - 1):
+            round_z_all(t)
+        quantize(nc, z2_codes[:], z2_scales[:], z2_grouped[:])
+
+        z_codes = keep.tile([P, H], U32, name="z_codes", align_bytes=64)
+        z_scales = keep.tile([P, H], U8, name="z_scales", align_bytes=64)
+        z_grouped = [keep.tile([P, P, PACK], BF16, name="z_grouped%d" % u, align_bytes=64) for u in range(PACK)]
+        for u in range(PACK):
+            round_z(PACK - 1, u)
+        for u in range(PACK):
+            cols = slice(u * P, (u + 1) * P)
+            nc.vector.tensor_copy(*weave_views(z_grouped[u][:], z_planes[:, :, cols]))
+            quantize(nc, z_codes[:, cols], z_scales[:, cols], z_grouped[u][:])
+
+        out_rows = out.rearrange("(p u) n -> p u n", u=PACK)
+        half = N // 2
+        for u in range(PACK):
+            cols = slice(u * P, (u + 1) * P)
+            cv_acc = psum.tile([P, N], F32, name="cv_acc", tag="first_chain", bufs=1)
+            product(nc, cv_acc[:], z_codes[:, cols], z_scales[:, cols], z2_codes[:], z2_scales[:])
+            cv = ring.tile([P, N], F32, name="cv")
+            minus_cv = ring.tile([P, N], F32, name="minus_cv")
+            if u == 0:
+                nc.vector.tensor_scalar(cv[:], cv_acc[:], 0.0625, None, ALU.mult)
+            else:
+                nc.scalar.activation(cv[:], cv_acc[:], ACT.Copy, scale=0.0625)
+            if u in (0, 1):
+                nc.vector.tensor_scalar(minus_cv[:], cv[:], -1.0, None, ALU.mult)
+            else:
+                nc.scalar.activation(minus_cv[:], cv_acc[:], ACT.Copy, scale=-0.0625)
+            gate = ring.tile([P, N], F32, name="gate")
+            diff = ring.tile([P, N], F32, name="diff")
+            result = ring.tile([P, N], F32, name="result")
+            for h in range(2):
+                cols = slice(h * half, (h + 1) * half)
+                entries = slice(h * half // 16, (h + 1) * half // 16)
+                nc.scalar.activation(gate[:, cols], cv[:].indirect(n4_t[:, entries]), ACT.Sigmoid)
+                nc.vector.tensor_tensor(diff[:, cols], minus_cv[:].indirect(n3_t[:, entries]), cv[:, cols], ALU.add)
+            for h in range(2):
+                cols = slice(h * half, (h + 1) * half)
+                nc.vector.tensor_tensor(result[:, cols], diff[:, cols], gate[:, cols], ALU.mult)
+                if u == PACK - 1:
+                    nc.sync.dma_start(out_rows[:, u, cols], result[:, cols])
+            if u < PACK - 1:
+                nc.sync.dma_start(out_rows[:, u, :], result[:])

@@ -111,25 +111,33 @@ def tile_picked_momhaargdif_none_p_kernel(
         xa_words = pick("xa_words", U32, table_words, offs_t)
         xb_words = pick("xb_words", U32, table_words, two_t)
 
-        a_acc = [psum.tile([P, H], F32, name="a_acc0", tag="first_chain", bufs=1)]
-        a_acc.extend(psum.tile([P, H], F32, name="a_acc%d" % t, tag="first", bufs=3) for t in range(1, PACK))
-        for t in range(PACK):
-            cols = slice(t * P, (t + 1) * P)
-            product(nc, a_acc[t][:], xa_words[:, cols], xa_scales[:, cols], wa_codes[:], wa_scales[:])
+        half = H // 2
+        a_first = [psum.tile([P, half], F32, name="a_first%d" % h, tag="chain%d" % h, bufs=1) for h in range(2)]
+        for h in range(2):
+            cols = slice(h * half, (h + 1) * half)
+            product(nc, a_first[h][:], xa_words[:, :P], xa_scales[:, :P], wa_codes[:, cols], wa_scales[:, cols])
 
         z_rows = [keep.tile([P, H], F32, name="z_rows%d" % t) for t in range(PACK)]
 
-        pa = [keep.tile([P, 2, W], F32, name="pa%d" % g) for g in range(2)]
-        minus_pb = [keep.tile([P, 2, W], F32, name="minus_pb%d" % g) for g in range(2)]
-        pair_sum = [keep.tile([P, 2, W], F32, name="pair_sum%d" % g) for g in range(2)]
+        groups = ((0,), (1,), (2, 3))
+        place = {t: (g, i) for g, members in enumerate(groups) for i, t in enumerate(members)}
+        pa = [keep.tile([P, len(m), W], F32, name="pa%d" % g) for g, m in enumerate(groups)]
+        minus_pb = [keep.tile([P, len(m), W], F32, name="minus_pb%d" % g) for g, m in enumerate(groups)]
+        pair_sum = [keep.tile([P, len(m), W], F32, name="pair_sum%d" % g) for g, m in enumerate(groups)]
+        a_tags = ("a_rows0", "a_rows1", "wb_raw1", "a_rows1")
+        acc_tags = ("", "chain0", "a_acc2", "a_acc3")
 
         def fetch_pairs(t):
-            g, i = divmod(t, 2)
-            if g == 0:
-                a_rows = keep.tile([P, H], F32, name="a_rows%d" % t)
+            g, i = place[t]
+            a_rows = keep.tile([P, H], F32, name="a_rows%d" % t, tag=a_tags[t])
+            if t == 0:
+                nc.scalar.activation(a_rows[:, :half], a_first[0][:], ACT.Copy, scale=gt_t[:, 0:1])
+                nc.vector.tensor_scalar(a_rows[:, half:], a_first[1][:], gt_t[:, 0:1], None, ALU.mult)
             else:
-                a_rows = keep.tile([P, H], F32, name="a_rows%d" % t, tag="wb_raw%d" % i)
-            nc.scalar.activation(a_rows[:], a_acc[t][:], ACT.Copy, scale=gt_t[:, t : t + 1])
+                cols = slice(t * P, (t + 1) * P)
+                a_acc = psum.tile([P, H], F32, name="a_acc", tag=acc_tags[t], bufs=1)
+                product(nc, a_acc[:], xa_words[:, cols], xa_scales[:, cols], wa_codes[:], wa_scales[:])
+                nc.scalar.activation(a_rows[:], a_acc[:], ACT.Copy, scale=gt_t[:, t : t + 1])
             nc.scalar.activation(pa[g][:, i, :], a_rows[:].indirect(n1_t[:]), ACT.Copy)
             if t == 0:
                 nc.vector.tensor_scalar(minus_pb[g][:, i, :], a_rows[:].indirect(n2_t[:]), -1.0, 0.0, ALU.mult, ALU.add)
@@ -137,34 +145,36 @@ def tile_picked_momhaargdif_none_p_kernel(
                 nc.scalar.activation(minus_pb[g][:, i, :], a_rows[:].indirect(n2_t[:]), ACT.Copy, scale=-1.0)
 
         def put_difference(t):
-            g, i = divmod(t, 2)
+            g, i = place[t]
             nc.vector.tensor_tensor(z_rows[t][:].indirect(n2_t[:]), pa[g][:, i, :], minus_pb[g][:, i, :], ALU.add)
 
-        scaled_pb = keep.tile([P, 2, W], F32, name="scaled_pb")
+        on_scalar = (2,)
+        scaled_pb = [keep.tile([P, len(m), W], F32, name="scaled_pb%d" % g) for g, m in enumerate(groups)]
 
         def put_sum(t):
-            g, i = divmod(t, 2)
-            other = scaled_pb[:, i, :] if g == 1 else three_quarters[:]
-            op = ALU.add if g == 1 else ALU.mult
+            g, i = place[t]
+            other = scaled_pb[g][:, i, :] if g in on_scalar else three_quarters[:]
+            op = ALU.add if g in on_scalar else ALU.mult
             nc.vector.tensor_tensor(z_rows[t][:].indirect(n1_t[:]), pair_sum[g][:, i, :], other, op)
 
         def put_pairs(g):
-            put_difference(2 * g)
-            if g == 1:
+            put_difference(groups[g][0])
+            if g in on_scalar:
                 nc.scalar.activation(pair_sum[g][:], pa[g][:], ACT.Copy, scale=0.75)
-                nc.scalar.activation(scaled_pb[:], minus_pb[g][:], ACT.Copy, scale=-0.75)
+                nc.scalar.activation(scaled_pb[g][:], minus_pb[g][:], ACT.Copy, scale=-0.75)
             else:
                 nc.vector.tensor_tensor(pair_sum[g][:], pa[g][:], minus_pb[g][:], ALU.subtract)
-            put_difference(2 * g + 1)
-            put_sum(2 * g)
-            put_sum(2 * g + 1)
+            for t in groups[g][1:]:
+                put_difference(t)
+            for t in groups[g]:
+                put_sum(t)
 
         def round_z(t, u):
             nc.scalar.copy(z_planes[:, t, u * P : (u + 1) * P], z_rows[t][:, u::PACK])
 
         def round_z_all(t):
             nc.scalar.copy(
-                z_planes[:, t, :].rearrange("p (u m) -> p u m", u=PACK), z_rows[t][:].rearrange("p (m u) -> p u m", u=PACK)
+                z_planes[:, t, :].rearrange("p (u m) -> p m u", u=PACK), z_rows[t][:].rearrange("p (m u) -> p m u", u=PACK)
             )
 
         wb_codes = keep.tile([P, N], U32, name="wb_codes", align_bytes=64)
@@ -196,11 +206,12 @@ def tile_picked_momhaargdif_none_p_kernel(
         prepare_wb(0)
         fetch_pairs(0)
         fetch_pairs(1)
-        prepare_wb(1)
         put_pairs(0)
+        prepare_wb(1)
+        put_pairs(1)
         fetch_pairs(2)
         fetch_pairs(3)
-        put_pairs(1)
+        put_pairs(2)
         make_z2(0)
         make_z2(1)
         z_planes = keep.tile([P, PACK, H], BF16, name="z_planes", tag="z2_planes")
@@ -219,29 +230,44 @@ def tile_picked_momhaargdif_none_p_kernel(
             quantize(nc, z_codes[:, cols], z_scales[:, cols], z_grouped[u][:])
 
         out_rows = out.rearrange("(p u) n -> p u n", u=PACK)
-        half = N // 2
         for u in range(PACK):
             cols = slice(u * P, (u + 1) * P)
-            cv_acc = psum.tile([P, N], F32, name="cv_acc", tag="first_chain", bufs=1)
-            product(nc, cv_acc[:], z_codes[:, cols], z_scales[:, cols], z2_codes[:], z2_scales[:])
             cv = ring.tile([P, N], F32, name="cv")
-            minus_cv = ring.tile([P, N], F32, name="minus_cv")
             if u == 0:
-                nc.vector.tensor_scalar(cv[:], cv_acc[:], 0.0625, None, ALU.mult)
+                for h in range(2):
+                    part = slice(h * half, (h + 1) * half)
+                    cv_acc = psum.tile([P, half], F32, name="cv_first", tag="chain%d" % h, bufs=1)
+                    product(nc, cv_acc[:], z_codes[:, cols], z_scales[:, cols], z2_codes[:, part], z2_scales[:, part])
+                    nc.vector.tensor_scalar(cv[:, part], cv_acc[:], 0.0625, None, ALU.mult)
             else:
+                cv_acc = psum.tile([P, N], F32, name="cv_acc", tag="chain1", bufs=1)
+                product(nc, cv_acc[:], z_codes[:, cols], z_scales[:, cols], z2_codes[:], z2_scales[:])
                 nc.scalar.activation(cv[:], cv_acc[:], ACT.Copy, scale=0.0625)
-            if u in (0, 1):
+            form = ("nv","nv","ns","ns")[u]
+            if form == "nv":
+                minus_cv = ring.tile([P, N], F32, name="minus_cv")
                 nc.vector.tensor_scalar(minus_cv[:], cv[:], -1.0, None, ALU.mult)
-            else:
+            if form == "ns":
+                minus_cv = ring.tile([P, N], F32, name="minus_cv")
                 nc.scalar.activation(minus_cv[:], cv_acc[:], ACT.Copy, scale=-0.0625)
             gate = ring.tile([P, N], F32, name="gate")
             diff = ring.tile([P, N], F32, name="diff")
             result = ring.tile([P, N], F32, name="result")
+            fetched = ring.tile([P, N], F32, name="fetched")
             for h in range(2):
                 cols = slice(h * half, (h + 1) * half)
                 entries = slice(h * half // 16, (h + 1) * half // 16)
+                if form == "ps" and h == 1:
+                    nc.scalar.activation(fetched[:, cols], cv[:].indirect(n3_t[:, entries]), ACT.Copy)
                 nc.scalar.activation(gate[:, cols], cv[:].indirect(n4_t[:, entries]), ACT.Sigmoid)
-                nc.vector.tensor_tensor(diff[:, cols], minus_cv[:].indirect(n3_t[:, entries]), cv[:, cols], ALU.add)
+                if form[0] == "n":
+                    nc.vector.tensor_tensor(diff[:, cols], minus_cv[:].indirect(n3_t[:, entries]), cv[:, cols], ALU.add)
+                elif form == "pv" or h == 0:
+                    nc.vector.tensor_copy(fetched[:, cols], cv[:].indirect(n3_t[:, entries]))
+            if form[0] == "p":
+                for h in range(2):
+                    cols = slice(h * half, (h + 1) * half)
+                    nc.vector.tensor_tensor(diff[:, cols], cv[:, cols], fetched[:, cols], ALU.subtract)
             for h in range(2):
                 cols = slice(h * half, (h + 1) * half)
                 nc.vector.tensor_tensor(result[:, cols], diff[:, cols], gate[:, cols], ALU.mult)

@@ -17,8 +17,14 @@ ACT = mybir.ActivationFunctionType
 
 P = 128
 PACK = 4
-WA_CHUNKS = ((0, 256), (256, 512))
-WB_CHUNKS = ((0, 256), (256, 512))
+QUADRANT = 32
+PER_COLUMN = 16
+HALVES = (slice(0, 256), slice(256, 512))
+HALF = 256
+
+PAIR_GROUPS = ((0,), (1,), (2, 3))
+TERMS_ON_SCALAR = 2
+NEGATE_ON_SCALAR_FROM = 2
 
 
 def weave_views(grouped, planes):
@@ -44,26 +50,30 @@ def product(nc, acc, lhs_codes, lhs_scales, rhs_codes, rhs_scales):
     )
 
 
+def stationary(t):
+    return slice(t * P, (t + 1) * P)
+
+
 def tile_picked_momhaargdif_none_p_kernel(
     tc, x_words, x_scales, wa, wb, gt, gi, offs, two, n1, n2, n3, n4, out
 ):
     nc = tc.nc
     with ExitStack() as ctx:
         keep = ctx.enter_context(tc.tile_pool(name="keep", bufs=1))
-        ring = ctx.enter_context(tc.tile_pool(name="ring", bufs=4))
-        psum = ctx.enter_context(tc.psum_pool(name="psum", bufs=4))
+        ring = ctx.enter_context(tc.tile_pool(name="ring", bufs=PACK))
+        psum = ctx.enter_context(tc.psum_pool(name="psum", bufs=PACK))
 
         def load_list(name, src):
             tile = keep.tile(list(src.shape), U16, name=name)
             nc.sync.dma_start(tile[:], src)
             return tile
 
-        def load_weights(name, w, c0, c1):
-            raw = keep.tile([P, PACK, c1 - c0], F32, name=name)
-            nc.sync.dma_start(raw[:], w.rearrange("(p j) c -> p j c", j=PACK)[:, :, c0:c1])
+        def load_weights(name, w, cols):
+            raw = keep.tile([P, PACK, HALF], F32, name=name)
+            nc.sync.dma_start(raw[:], w.rearrange("(p j) c -> p j c", j=PACK)[:, :, cols])
             return raw
 
-        def load_column(name, g):
+        def load_place_weights(name, g):
             tile = keep.tile([P, PACK], F32, name=name)
             nc.sync.dma_start(tile[:], g.rearrange("(p t) o -> p (t o)", t=PACK))
             return tile
@@ -71,73 +81,66 @@ def tile_picked_momhaargdif_none_p_kernel(
         table_scales = keep.tile([P, T], U8, name="table_scales")
         nc.vector.memset(table_scales[:].bitcast(I32), 0)
         offs_t = load_list("offs_t", offs)
-        wa_raw = [load_weights("wa_raw0", wa, *WA_CHUNKS[0])]
-        for q in range(4):
+        wa_raw = [load_weights("wa_raw0", wa, HALVES[0])]
+        for q in range(P // QUADRANT):
             nc.sync.dma_start(
-                table_scales[32 * q : 32 * q + 4, :].bitcast(I32), x_scales[0, 4 * q : 4 * q + 4, :].bitcast(I32)
+                table_scales[QUADRANT * q : QUADRANT * q + PACK, :].bitcast(I32),
+                x_scales[0, PACK * q : PACK * (q + 1), :].bitcast(I32),
             )
-        wa_raw.append(load_weights("wa_raw1", wa, *WA_CHUNKS[1]))
+        wa_raw.append(load_weights("wa_raw1", wa, HALVES[1]))
         two_t = load_list("two_t", two)
         table_words = keep.tile([P, T], U32, name="table_words")
         nc.sync.dma_start(table_words[:].bitcast(I32), x_words[0].rearrange("p n t -> p (n t)").bitcast(I32))
-        wb_raw = [load_weights("wb_raw0", wb, *WB_CHUNKS[0])]
-        gt_t = load_column("gt_t", gt)
+        wb_raw = [load_weights("wb_raw0", wb, HALVES[0])]
+        gt_t = load_place_weights("gt_t", gt)
         n1_t = load_list("n1_t", n1)
         n2_t = load_list("n2_t", n2)
-        wb_raw.append(load_weights("wb_raw1", wb, *WB_CHUNKS[1]))
-        gi_t = load_column("gi_t", gi)
+        wb_raw.append(load_weights("wb_raw1", wb, HALVES[1]))
+        gi_t = load_place_weights("gi_t", gi)
         n3_t = load_list("n3_t", n3)
         n4_t = load_list("n4_t", n4)
         three_quarters = keep.tile([P, W], F32, name="three_quarters")
         nc.gpsimd.memset(three_quarters[:], 0.75)
 
-        def pick(name, dtype, table, lst):
+        def pick(name, dtype, table, offsets):
             tile = keep.tile([P, S], dtype, name=name, align_bytes=64)
-            nc.vector.tensor_copy(tile[:].rearrange("p (t m) -> p m t", t=PACK), table[:].indirect(lst[:]))
+            nc.vector.tensor_copy(tile[:].rearrange("p (t m) -> p m t", t=PACK), table[:].indirect(offsets[:]))
             return tile
 
         wa_codes = keep.tile([P, H], U32, name="wa_codes", align_bytes=64)
         wa_scales = keep.tile([P, H], U8, name="wa_scales", align_bytes=64)
-        wa_grouped = [
-            keep.tile([P, c1 - c0, PACK], BF16, name="wa_grouped%d" % c, align_bytes=64)
-            for c, (c0, c1) in enumerate(WA_CHUNKS)
-        ]
-        for c in range(len(WA_CHUNKS)):
-            nc.scalar.copy(*weave_views(wa_grouped[c][:], wa_raw[c][:]))
+        wa_grouped = [keep.tile([P, HALF, PACK], BF16, name="wa_grouped%d" % h, align_bytes=64) for h in range(2)]
+        for h in range(2):
+            nc.scalar.copy(*weave_views(wa_grouped[h][:], wa_raw[h][:]))
         xa_scales = pick("xa_scales", U8, table_scales, offs_t)
         xb_scales = pick("xb_scales", U8, table_scales, two_t)
-        for c, (c0, c1) in enumerate(WA_CHUNKS):
-            quantize(nc, wa_codes[:, c0:c1], wa_scales[:, c0:c1], wa_grouped[c][:])
+        for h, cols in enumerate(HALVES):
+            quantize(nc, wa_codes[:, cols], wa_scales[:, cols], wa_grouped[h][:])
         xa_words = pick("xa_words", U32, table_words, offs_t)
         xb_words = pick("xb_words", U32, table_words, two_t)
 
-        half = H // 2
-        a_first = [psum.tile([P, half], F32, name="a_first%d" % h, tag="chain%d" % h, bufs=1) for h in range(2)]
-        for h in range(2):
-            cols = slice(h * half, (h + 1) * half)
+        a_first = [psum.tile([P, HALF], F32, name="a_first%d" % h, tag="shared_bank%d" % h, bufs=1) for h in range(2)]
+        for h, cols in enumerate(HALVES):
             product(nc, a_first[h][:], xa_words[:, :P], xa_scales[:, :P], wa_codes[:, cols], wa_scales[:, cols])
 
         z_rows = [keep.tile([P, H], F32, name="z_rows%d" % t) for t in range(PACK)]
-
-        groups = ((0,), (1,), (2, 3))
-        place = {t: (g, i) for g, members in enumerate(groups) for i, t in enumerate(members)}
-        pa = [keep.tile([P, len(m), W], F32, name="pa%d" % g) for g, m in enumerate(groups)]
-        minus_pb = [keep.tile([P, len(m), W], F32, name="minus_pb%d" % g) for g, m in enumerate(groups)]
-        pair_sum = [keep.tile([P, len(m), W], F32, name="pair_sum%d" % g) for g, m in enumerate(groups)]
-        a_tags = ("a_rows0", "a_rows1", "wb_raw1", "a_rows1")
-        acc_tags = ("", "chain0", "a_acc2", "a_acc3")
+        slot = {t: (g, i) for g, members in enumerate(PAIR_GROUPS) for i, t in enumerate(members)}
+        pa = [keep.tile([P, len(m), W], F32, name="pa%d" % g) for g, m in enumerate(PAIR_GROUPS)]
+        minus_pb = [keep.tile([P, len(m), W], F32, name="minus_pb%d" % g) for g, m in enumerate(PAIR_GROUPS)]
+        a_buffers = ("a_rows0", "a_rows1", "wb_raw1", "a_rows1")
+        a_banks = {1: "shared_bank0", 2: "a_bank2", 3: "a_bank3"}
 
         def fetch_pairs(t):
-            g, i = place[t]
-            a_rows = keep.tile([P, H], F32, name="a_rows%d" % t, tag=a_tags[t])
+            g, i = slot[t]
+            a_rows = keep.tile([P, H], F32, name="a_rows%d" % t, tag=a_buffers[t])
+            weight = gt_t[:, t : t + 1]
             if t == 0:
-                nc.scalar.activation(a_rows[:, :half], a_first[0][:], ACT.Copy, scale=gt_t[:, 0:1])
-                nc.vector.tensor_scalar(a_rows[:, half:], a_first[1][:], gt_t[:, 0:1], None, ALU.mult)
+                nc.scalar.activation(a_rows[:, HALVES[0]], a_first[0][:], ACT.Copy, scale=weight)
+                nc.vector.tensor_scalar(a_rows[:, HALVES[1]], a_first[1][:], weight, None, ALU.mult)
             else:
-                cols = slice(t * P, (t + 1) * P)
-                a_acc = psum.tile([P, H], F32, name="a_acc", tag=acc_tags[t], bufs=1)
-                product(nc, a_acc[:], xa_words[:, cols], xa_scales[:, cols], wa_codes[:], wa_scales[:])
-                nc.scalar.activation(a_rows[:], a_acc[:], ACT.Copy, scale=gt_t[:, t : t + 1])
+                a_acc = psum.tile([P, H], F32, name="a_acc", tag=a_banks[t], bufs=1)
+                product(nc, a_acc[:], xa_words[:, stationary(t)], xa_scales[:, stationary(t)], wa_codes[:], wa_scales[:])
+                nc.scalar.activation(a_rows[:], a_acc[:], ACT.Copy, scale=weight)
             nc.scalar.activation(pa[g][:, i, :], a_rows[:].indirect(n1_t[:]), ACT.Copy)
             if t == 0:
                 nc.vector.tensor_scalar(minus_pb[g][:, i, :], a_rows[:].indirect(n2_t[:]), -1.0, 0.0, ALU.mult, ALU.add)
@@ -145,63 +148,47 @@ def tile_picked_momhaargdif_none_p_kernel(
                 nc.scalar.activation(minus_pb[g][:, i, :], a_rows[:].indirect(n2_t[:]), ACT.Copy, scale=-1.0)
 
         def put_difference(t):
-            g, i = place[t]
+            g, i = slot[t]
             nc.vector.tensor_tensor(z_rows[t][:].indirect(n2_t[:]), pa[g][:, i, :], minus_pb[g][:, i, :], ALU.add)
 
-        on_scalar = (2,)
-        scaled_pb = [keep.tile([P, len(m), W], F32, name="scaled_pb%d" % g) for g, m in enumerate(groups)]
-
-        def put_sum(t):
-            g, i = place[t]
-            other = scaled_pb[g][:, i, :] if g in on_scalar else three_quarters[:]
-            op = ALU.add if g in on_scalar else ALU.mult
-            nc.vector.tensor_tensor(z_rows[t][:].indirect(n1_t[:]), pair_sum[g][:, i, :], other, op)
-
         def put_pairs(g):
-            put_difference(groups[g][0])
-            if g in on_scalar:
-                nc.scalar.activation(pair_sum[g][:], pa[g][:], ACT.Copy, scale=0.75)
-                nc.scalar.activation(scaled_pb[g][:], minus_pb[g][:], ACT.Copy, scale=-0.75)
+            members = PAIR_GROUPS[g]
+            shape = [P, len(members), W]
+            put_difference(members[0])
+            if g == TERMS_ON_SCALAR:
+                pa_term = keep.tile(shape, F32, name="pa_term")
+                pb_term = keep.tile(shape, F32, name="pb_term")
+                nc.scalar.activation(pa_term[:], pa[g][:], ACT.Copy, scale=0.75)
+                nc.scalar.activation(pb_term[:], minus_pb[g][:], ACT.Copy, scale=-0.75)
+                operands = [(pa_term[:, i, :], pb_term[:, i, :], ALU.add) for i in range(len(members))]
             else:
-                nc.vector.tensor_tensor(pair_sum[g][:], pa[g][:], minus_pb[g][:], ALU.subtract)
-            for t in groups[g][1:]:
+                pair_sum = keep.tile(shape, F32, name="pair_sum%d" % g)
+                nc.vector.tensor_tensor(pair_sum[:], pa[g][:], minus_pb[g][:], ALU.subtract)
+                operands = [(pair_sum[:, i, :], three_quarters[:], ALU.mult) for i in range(len(members))]
+            for t in members[1:]:
                 put_difference(t)
-            for t in groups[g]:
-                put_sum(t)
-
-        def round_z(t, u):
-            nc.scalar.copy(z_planes[:, t, u * P : (u + 1) * P], z_rows[t][:, u::PACK])
-
-        def round_z_all(t):
-            nc.scalar.copy(
-                z_planes[:, t, :].rearrange("p (u m) -> p m u", u=PACK), z_rows[t][:].rearrange("p (m u) -> p m u", u=PACK)
-            )
+            for t, (in0, in1, op) in zip(members, operands):
+                nc.vector.tensor_tensor(z_rows[t][:].indirect(n1_t[:]), in0, in1, op)
 
         wb_codes = keep.tile([P, N], U32, name="wb_codes", align_bytes=64)
         wb_scales = keep.tile([P, N], U8, name="wb_scales", align_bytes=64)
-        wb_grouped = [
-            keep.tile([P, c1 - c0, PACK], BF16, name="wb_grouped%d" % c, align_bytes=64)
-            for c, (c0, c1) in enumerate(WB_CHUNKS)
-        ]
-        b_acc = [psum.tile([P, N], F32, name="b_acc%d" % t, tag="second") for t in range(PACK)]
-
-        def prepare_wb(c):
-            c0, c1 = WB_CHUNKS[c]
-            nc.scalar.copy(*weave_views(wb_grouped[c][:], wb_raw[c][:]))
-            quantize(nc, wb_codes[:, c0:c1], wb_scales[:, c0:c1], wb_grouped[c][:])
-
-        def make_z2(c):
-            c0, c1 = WB_CHUNKS[c]
-            for t in range(PACK):
-                cols = slice(t * P, (t + 1) * P)
-                product(nc, b_acc[t][:, c0:c1], xb_words[:, cols], xb_scales[:, cols], wb_codes[:, c0:c1], wb_scales[:, c0:c1])
-                nc.scalar.activation(z2_planes[:, t, c0:c1], b_acc[t][:, c0:c1], ACT.Copy, scale=gi_t[:, t : t + 1])
-            nc.scalar.copy(*weave_views(z2_grouped[:, c0:c1, :], z2_planes[:, :, c0:c1]))
-
+        wb_grouped = [keep.tile([P, HALF, PACK], BF16, name="wb_grouped%d" % h, align_bytes=64) for h in range(2)]
+        b_acc = [psum.tile([P, N], F32, name="b_acc%d" % t, tag="b_banks") for t in range(PACK)]
         z2_planes = keep.tile([P, PACK, N], BF16, name="z2_planes")
         z2_grouped = keep.tile([P, N, PACK], BF16, name="z2_grouped", align_bytes=64)
         z2_codes = keep.tile([P, N], U32, name="z2_codes", align_bytes=64)
         z2_scales = keep.tile([P, N], U8, name="z2_scales", align_bytes=64)
+
+        def prepare_wb(h):
+            nc.scalar.copy(*weave_views(wb_grouped[h][:], wb_raw[h][:]))
+            quantize(nc, wb_codes[:, HALVES[h]], wb_scales[:, HALVES[h]], wb_grouped[h][:])
+
+        def make_z2(cols):
+            for t in range(PACK):
+                acc = b_acc[t][:, cols]
+                product(nc, acc, xb_words[:, stationary(t)], xb_scales[:, stationary(t)], wb_codes[:, cols], wb_scales[:, cols])
+                nc.scalar.activation(z2_planes[:, t, cols], acc, ACT.Copy, scale=gi_t[:, t : t + 1])
+            nc.scalar.copy(*weave_views(z2_grouped[:, cols, :], z2_planes[:, :, cols]))
 
         prepare_wb(0)
         fetch_pairs(0)
@@ -212,66 +199,55 @@ def tile_picked_momhaargdif_none_p_kernel(
         fetch_pairs(2)
         fetch_pairs(3)
         put_pairs(2)
-        make_z2(0)
-        make_z2(1)
+        for cols in HALVES:
+            make_z2(cols)
+
         z_planes = keep.tile([P, PACK, H], BF16, name="z_planes", tag="z2_planes")
         for t in range(PACK - 1):
-            round_z_all(t)
+            nc.scalar.copy(
+                z_planes[:, t, :].rearrange("p (u m) -> p m u", u=PACK),
+                z_rows[t][:].rearrange("p (m u) -> p m u", u=PACK),
+            )
         quantize(nc, z2_codes[:], z2_scales[:], z2_grouped[:])
 
         z_codes = keep.tile([P, H], U32, name="z_codes", align_bytes=64)
         z_scales = keep.tile([P, H], U8, name="z_scales", align_bytes=64)
         z_grouped = [keep.tile([P, P, PACK], BF16, name="z_grouped%d" % u, align_bytes=64) for u in range(PACK)]
         for u in range(PACK):
-            round_z(PACK - 1, u)
+            nc.scalar.copy(z_planes[:, PACK - 1, stationary(u)], z_rows[PACK - 1][:, u::PACK])
         for u in range(PACK):
-            cols = slice(u * P, (u + 1) * P)
-            nc.vector.tensor_copy(*weave_views(z_grouped[u][:], z_planes[:, :, cols]))
-            quantize(nc, z_codes[:, cols], z_scales[:, cols], z_grouped[u][:])
+            nc.vector.tensor_copy(*weave_views(z_grouped[u][:], z_planes[:, :, stationary(u)]))
+            quantize(nc, z_codes[:, stationary(u)], z_scales[:, stationary(u)], z_grouped[u][:])
 
         out_rows = out.rearrange("(p u) n -> p u n", u=PACK)
         for u in range(PACK):
-            cols = slice(u * P, (u + 1) * P)
+            lhs = (z_codes[:, stationary(u)], z_scales[:, stationary(u)])
             cv = ring.tile([P, N], F32, name="cv")
             if u == 0:
-                for h in range(2):
-                    part = slice(h * half, (h + 1) * half)
-                    cv_acc = psum.tile([P, half], F32, name="cv_first", tag="chain%d" % h, bufs=1)
-                    product(nc, cv_acc[:], z_codes[:, cols], z_scales[:, cols], z2_codes[:, part], z2_scales[:, part])
-                    nc.vector.tensor_scalar(cv[:, part], cv_acc[:], 0.0625, None, ALU.mult)
+                for h, cols in enumerate(HALVES):
+                    cv_first = psum.tile([P, HALF], F32, name="cv_first", tag="shared_bank%d" % h, bufs=1)
+                    product(nc, cv_first[:], *lhs, z2_codes[:, cols], z2_scales[:, cols])
+                    nc.vector.tensor_scalar(cv[:, cols], cv_first[:], 0.0625, None, ALU.mult)
             else:
-                cv_acc = psum.tile([P, N], F32, name="cv_acc", tag="chain1", bufs=1)
-                product(nc, cv_acc[:], z_codes[:, cols], z_scales[:, cols], z2_codes[:], z2_scales[:])
+                cv_acc = psum.tile([P, N], F32, name="cv_acc", tag="shared_bank1", bufs=1)
+                product(nc, cv_acc[:], *lhs, z2_codes[:], z2_scales[:])
                 nc.scalar.activation(cv[:], cv_acc[:], ACT.Copy, scale=0.0625)
-            form = ("nv","nv","ns","ns")[u]
-            if form == "nv":
-                minus_cv = ring.tile([P, N], F32, name="minus_cv")
+            minus_cv = ring.tile([P, N], F32, name="minus_cv")
+            if u < NEGATE_ON_SCALAR_FROM:
                 nc.vector.tensor_scalar(minus_cv[:], cv[:], -1.0, None, ALU.mult)
-            if form == "ns":
-                minus_cv = ring.tile([P, N], F32, name="minus_cv")
+            else:
                 nc.scalar.activation(minus_cv[:], cv_acc[:], ACT.Copy, scale=-0.0625)
             gate = ring.tile([P, N], F32, name="gate")
             diff = ring.tile([P, N], F32, name="diff")
             result = ring.tile([P, N], F32, name="result")
-            fetched = ring.tile([P, N], F32, name="fetched")
-            for h in range(2):
-                cols = slice(h * half, (h + 1) * half)
-                entries = slice(h * half // 16, (h + 1) * half // 16)
-                if form == "ps" and h == 1:
-                    nc.scalar.activation(fetched[:, cols], cv[:].indirect(n3_t[:, entries]), ACT.Copy)
+            for cols in HALVES:
+                entries = slice(cols.start // PER_COLUMN, cols.stop // PER_COLUMN)
                 nc.scalar.activation(gate[:, cols], cv[:].indirect(n4_t[:, entries]), ACT.Sigmoid)
-                if form[0] == "n":
-                    nc.vector.tensor_tensor(diff[:, cols], minus_cv[:].indirect(n3_t[:, entries]), cv[:, cols], ALU.add)
-                elif form == "pv" or h == 0:
-                    nc.vector.tensor_copy(fetched[:, cols], cv[:].indirect(n3_t[:, entries]))
-            if form[0] == "p":
-                for h in range(2):
-                    cols = slice(h * half, (h + 1) * half)
-                    nc.vector.tensor_tensor(diff[:, cols], cv[:, cols], fetched[:, cols], ALU.subtract)
-            for h in range(2):
-                cols = slice(h * half, (h + 1) * half)
+                nc.vector.tensor_tensor(diff[:, cols], minus_cv[:].indirect(n3_t[:, entries]), cv[:, cols], ALU.add)
+            last = u == PACK - 1
+            for cols in HALVES:
                 nc.vector.tensor_tensor(result[:, cols], diff[:, cols], gate[:, cols], ALU.mult)
-                if u == PACK - 1:
+                if last:
                     nc.sync.dma_start(out_rows[:, u, cols], result[:, cols])
-            if u < PACK - 1:
+            if not last:
                 nc.sync.dma_start(out_rows[:, u, :], result[:])

from contextlib import ExitStack

import concourse.mybir as mybir

K, T, S, N, H, W = 512, 2048, 512, 512, 512, 256
FLOPS = 2 * K * S * H + 2 * K * S * N + 2 * S * H * N

F32 = mybir.dt.float32
BF16 = mybir.dt.bfloat16
I32 = mybir.dt.int32
U32 = mybir.dt.uint32
U16 = mybir.dt.uint16
U8 = mybir.dt.uint8
FP8X4 = mybir.dt.float8_e4m3fn_x4
ALU = mybir.AluOpType
ACT = mybir.ActivationFunctionType

P = 128
PACK = 4
QUADRANT = 32
PER_COLUMN = 16
HALVES = (slice(0, 256), slice(256, 512))
HALF = 256

PAIR_GROUPS = ((0,), (1,), (2, 3))
TERMS_ON_SCALAR = 2
NEGATE_ON_SCALAR_FROM = 2


def weave_views(grouped, planes):
    return (
        grouped.rearrange("p (c i) j -> p c j i", i=PACK),
        planes.rearrange("p j (c i) -> p c j i", i=PACK),
    )


def quantize(nc, codes, scales, grouped):
    nc.vector.quantize_mx(out=codes.bitcast(FP8X4), scales=scales, in_=grouped.rearrange("p c j -> p (c j)"))


def product(nc, acc, lhs_codes, lhs_scales, rhs_codes, rhs_scales):
    nc.tensor.matmul_mx(
        out=acc,
        lhsT=lhs_codes.bitcast(FP8X4),
        lhsT_scale=lhs_scales,
        rhs=rhs_codes.bitcast(FP8X4),
        rhs_scale=rhs_scales,
        start=True,
        stop=True,
    )


def stationary(t):
    return slice(t * P, (t + 1) * P)


def tile_picked_momhaargdif_none_p_kernel(
    tc, x_words, x_scales, wa, wb, gt, gi, offs, two, n1, n2, n3, n4, out
):
    nc = tc.nc
    with ExitStack() as ctx:
        keep = ctx.enter_context(tc.tile_pool(name="keep", bufs=1))
        ring = ctx.enter_context(tc.tile_pool(name="ring", bufs=PACK))
        psum = ctx.enter_context(tc.psum_pool(name="psum", bufs=PACK))

        def load_list(name, src):
            tile = keep.tile(list(src.shape), U16, name=name)
            nc.sync.dma_start(tile[:], src)
            return tile

        def load_weights(name, w, cols):
            raw = keep.tile([P, PACK, HALF], F32, name=name)
            nc.sync.dma_start(raw[:], w.rearrange("(p j) c -> p j c", j=PACK)[:, :, cols])
            return raw

        def load_place_weights(name, g):
            tile = keep.tile([P, PACK], F32, name=name)
            nc.sync.dma_start(tile[:], g.rearrange("(p t) o -> p (t o)", t=PACK))
            return tile

        table_scales = keep.tile([P, T], U8, name="table_scales")
        nc.vector.memset(table_scales[:].bitcast(I32), 0)
        offs_t = load_list("offs_t", offs)
        wa_raw = [load_weights("wa_raw0", wa, HALVES[0])]
        for q in range(P // QUADRANT):
            nc.sync.dma_start(
                table_scales[QUADRANT * q : QUADRANT * q + PACK, :].bitcast(I32),
                x_scales[0, PACK * q : PACK * (q + 1), :].bitcast(I32),
            )
        wa_raw.append(load_weights("wa_raw1", wa, HALVES[1]))
        two_t = load_list("two_t", two)
        table_words = keep.tile([P, T], U32, name="table_words")
        nc.sync.dma_start(table_words[:].bitcast(I32), x_words[0].rearrange("p n t -> p (n t)").bitcast(I32))
        wb_raw = [load_weights("wb_raw0", wb, HALVES[0])]
        gt_t = load_place_weights("gt_t", gt)
        n1_t = load_list("n1_t", n1)
        n2_t = load_list("n2_t", n2)
        wb_raw.append(load_weights("wb_raw1", wb, HALVES[1]))
        gi_t = load_place_weights("gi_t", gi)
        n3_t = load_list("n3_t", n3)
        n4_t = load_list("n4_t", n4)
        three_quarters = keep.tile([P, W], F32, name="three_quarters")
        nc.gpsimd.memset(three_quarters[:], 0.75)

        def pick(name, dtype, table, offsets):
            tile = keep.tile([P, S], dtype, name=name, align_bytes=64)
            nc.vector.tensor_copy(tile[:].rearrange("p (t m) -> p m t", t=PACK), table[:].indirect(offsets[:]))
            return tile

        wa_codes = keep.tile([P, H], U32, name="wa_codes", align_bytes=64)
        wa_scales = keep.tile([P, H], U8, name="wa_scales", align_bytes=64)
        wa_grouped = [keep.tile([P, HALF, PACK], BF16, name="wa_grouped%d" % h, align_bytes=64) for h in range(2)]
        for h in range(2):
            nc.scalar.copy(*weave_views(wa_grouped[h][:], wa_raw[h][:]))
        xa_scales = pick("xa_scales", U8, table_scales, offs_t)
        xb_scales = pick("xb_scales", U8, table_scales, two_t)
        for h, cols in enumerate(HALVES):
            quantize(nc, wa_codes[:, cols], wa_scales[:, cols], wa_grouped[h][:])
        xa_words = pick("xa_words", U32, table_words, offs_t)
        xb_words = pick("xb_words", U32, table_words, two_t)

        a_first = [psum.tile([P, HALF], F32, name="a_first%d" % h, tag="shared_bank%d" % h, bufs=1) for h in range(2)]
        for h, cols in enumerate(HALVES):
            product(nc, a_first[h][:], xa_words[:, :P], xa_scales[:, :P], wa_codes[:, cols], wa_scales[:, cols])

        z_rows = [keep.tile([P, H], F32, name="z_rows%d" % t) for t in range(PACK)]
        slot = {t: (g, i) for g, members in enumerate(PAIR_GROUPS) for i, t in enumerate(members)}
        pa = [keep.tile([P, len(m), W], F32, name="pa%d" % g) for g, m in enumerate(PAIR_GROUPS)]
        minus_pb = [keep.tile([P, len(m), W], F32, name="minus_pb%d" % g) for g, m in enumerate(PAIR_GROUPS)]
        a_buffers = ("a_rows0", "a_rows1", "wb_raw1", "a_rows1")
        a_banks = {1: "shared_bank0", 2: "a_bank2", 3: "a_bank3"}

        def fetch_pairs(t):
            g, i = slot[t]
            a_rows = keep.tile([P, H], F32, name="a_rows%d" % t, tag=a_buffers[t])
            weight = gt_t[:, t : t + 1]
            if t == 0:
                nc.scalar.activation(a_rows[:, HALVES[0]], a_first[0][:], ACT.Copy, scale=weight)
                nc.vector.tensor_scalar(a_rows[:, HALVES[1]], a_first[1][:], weight, None, ALU.mult)
            else:
                a_acc = psum.tile([P, H], F32, name="a_acc", tag=a_banks[t], bufs=1)
                product(nc, a_acc[:], xa_words[:, stationary(t)], xa_scales[:, stationary(t)], wa_codes[:], wa_scales[:])
                nc.scalar.activation(a_rows[:], a_acc[:], ACT.Copy, scale=weight)
            nc.scalar.activation(pa[g][:, i, :], a_rows[:].indirect(n1_t[:]), ACT.Copy)
            if t == 0:
                nc.vector.tensor_scalar(minus_pb[g][:, i, :], a_rows[:].indirect(n2_t[:]), -1.0, 0.0, ALU.mult, ALU.add)
            else:
                nc.scalar.activation(minus_pb[g][:, i, :], a_rows[:].indirect(n2_t[:]), ACT.Copy, scale=-1.0)

        def put_difference(t):
            g, i = slot[t]
            nc.vector.tensor_tensor(z_rows[t][:].indirect(n2_t[:]), pa[g][:, i, :], minus_pb[g][:, i, :], ALU.add)

        def put_pairs(g):
            members = PAIR_GROUPS[g]
            shape = [P, len(members), W]
            put_difference(members[0])
            if g == TERMS_ON_SCALAR:
                pa_term = keep.tile(shape, F32, name="pa_term")
                pb_term = keep.tile(shape, F32, name="pb_term")
                nc.scalar.activation(pa_term[:], pa[g][:], ACT.Copy, scale=0.75)
                nc.scalar.activation(pb_term[:], minus_pb[g][:], ACT.Copy, scale=-0.75)
                operands = [(pa_term[:, i, :], pb_term[:, i, :], ALU.add) for i in range(len(members))]
            else:
                pair_sum = keep.tile(shape, F32, name="pair_sum%d" % g)
                nc.vector.tensor_tensor(pair_sum[:], pa[g][:], minus_pb[g][:], ALU.subtract)
                operands = [(pair_sum[:, i, :], three_quarters[:], ALU.mult) for i in range(len(members))]
            for t in members[1:]:
                put_difference(t)
            for t, (in0, in1, op) in zip(members, operands):
                nc.vector.tensor_tensor(z_rows[t][:].indirect(n1_t[:]), in0, in1, op)

        wb_codes = keep.tile([P, N], U32, name="wb_codes", align_bytes=64)
        wb_scales = keep.tile([P, N], U8, name="wb_scales", align_bytes=64)
        wb_grouped = [keep.tile([P, HALF, PACK], BF16, name="wb_grouped%d" % h, align_bytes=64) for h in range(2)]
        b_acc = [psum.tile([P, N], F32, name="b_acc%d" % t, tag="b_banks") for t in range(PACK)]
        z2_planes = keep.tile([P, PACK, N], BF16, name="z2_planes")
        z2_grouped = keep.tile([P, N, PACK], BF16, name="z2_grouped", align_bytes=64)
        z2_codes = keep.tile([P, N], U32, name="z2_codes", align_bytes=64)
        z2_scales = keep.tile([P, N], U8, name="z2_scales", align_bytes=64)

        def prepare_wb(h):
            nc.scalar.copy(*weave_views(wb_grouped[h][:], wb_raw[h][:]))
            quantize(nc, wb_codes[:, HALVES[h]], wb_scales[:, HALVES[h]], wb_grouped[h][:])

        def make_z2(cols):
            for t in range(PACK):
                acc = b_acc[t][:, cols]
                product(nc, acc, xb_words[:, stationary(t)], xb_scales[:, stationary(t)], wb_codes[:, cols], wb_scales[:, cols])
                nc.scalar.activation(z2_planes[:, t, cols], acc, ACT.Copy, scale=gi_t[:, t : t + 1])
            nc.scalar.copy(*weave_views(z2_grouped[:, cols, :], z2_planes[:, :, cols]))

        prepare_wb(0)
        fetch_pairs(0)
        fetch_pairs(1)
        put_pairs(0)
        prepare_wb(1)
        put_pairs(1)
        fetch_pairs(2)
        fetch_pairs(3)
        put_pairs(2)
        for cols in HALVES:
            make_z2(cols)

        z_planes = keep.tile([P, PACK, H], BF16, name="z_planes", tag="z2_planes")
        for t in range(PACK - 1):
            nc.scalar.copy(
                z_planes[:, t, :].rearrange("p (u m) -> p m u", u=PACK),
                z_rows[t][:].rearrange("p (m u) -> p m u", u=PACK),
            )
        quantize(nc, z2_codes[:], z2_scales[:], z2_grouped[:])

        z_codes = keep.tile([P, H], U32, name="z_codes", align_bytes=64)
        z_scales = keep.tile([P, H], U8, name="z_scales", align_bytes=64)
        z_grouped = [keep.tile([P, P, PACK], BF16, name="z_grouped%d" % u, align_bytes=64) for u in range(PACK)]
        for u in range(PACK):
            nc.scalar.copy(z_planes[:, PACK - 1, stationary(u)], z_rows[PACK - 1][:, u::PACK])
        for u in range(PACK):
            nc.vector.tensor_copy(*weave_views(z_grouped[u][:], z_planes[:, :, stationary(u)]))
            quantize(nc, z_codes[:, stationary(u)], z_scales[:, stationary(u)], z_grouped[u][:])

        out_rows = out.rearrange("(p u) n -> p u n", u=PACK)
        for u in range(PACK):
            lhs = (z_codes[:, stationary(u)], z_scales[:, stationary(u)])
            cv = ring.tile([P, N], F32, name="cv")
            if u == 0:
                for h, cols in enumerate(HALVES):
                    cv_first = psum.tile([P, HALF], F32, name="cv_first", tag="shared_bank%d" % h, bufs=1)
                    product(nc, cv_first[:], *lhs, z2_codes[:, cols], z2_scales[:, cols])
                    nc.vector.tensor_scalar(cv[:, cols], cv_first[:], 0.0625, None, ALU.mult)
            else:
                cv_acc = psum.tile([P, N], F32, name="cv_acc", tag="shared_bank1", bufs=1)
                product(nc, cv_acc[:], *lhs, z2_codes[:], z2_scales[:])
                nc.scalar.activation(cv[:], cv_acc[:], ACT.Copy, scale=0.0625)
            minus_cv = ring.tile([P, N], F32, name="minus_cv")
            if u < NEGATE_ON_SCALAR_FROM:
                nc.vector.tensor_scalar(minus_cv[:], cv[:], -1.0, None, ALU.mult)
            else:
                nc.scalar.activation(minus_cv[:], cv_acc[:], ACT.Copy, scale=-0.0625)
            gate = ring.tile([P, N], F32, name="gate")
            diff = ring.tile([P, N], F32, name="diff")
            result = ring.tile([P, N], F32, name="result")
            for cols in HALVES:
                entries = slice(cols.start // PER_COLUMN, cols.stop // PER_COLUMN)
                nc.scalar.activation(gate[:, cols], cv[:].indirect(n4_t[:, entries]), ACT.Sigmoid)
                nc.vector.tensor_tensor(diff[:, cols], minus_cv[:].indirect(n3_t[:, entries]), cv[:, cols], ALU.add)
            last = u == PACK - 1
            for cols in HALVES:
                nc.vector.tensor_tensor(result[:, cols], diff[:, cols], gate[:, cols], ALU.mult)
                if last:
                    nc.sync.dma_start(out_rows[:, u, cols], result[:, cols])
            if not last:
                nc.sync.dma_start(out_rows[:, u, :], result[:])
